import numpy as np
import ml_dtypes


def mxq(x, axis, fmt="e4m3"):
    dtype, down = {"e4m3": (ml_dtypes.float8_e4m3fn, 7), "e5m2": (ml_dtypes.float8_e5m2, 14)}[fmt]
    v = np.moveaxis(np.asarray(x, np.float32).astype(ml_dtypes.bfloat16).astype(np.float64), axis, -1)
    blocks = v.reshape(v.shape[:-1] + (-1, 32))
    amax = np.abs(blocks).max(-1, keepdims=True)
    byte = np.maximum(np.where(amax > 0, np.frexp(amax)[1] - 1 + 127, 0) - down, 1)
    scale = np.exp2(byte - 127.0)
    codes = (blocks / scale).astype(np.float32).astype(dtype).astype(np.float64)
    return np.moveaxis((codes * scale).reshape(v.shape), -1, axis)


WIDE = False


def mx_kscale(k):
    if not WIDE:
        return np.ones(k)
    levels = np.array([10, -10, 5, -5, 0])
    if k % 512:
        return np.exp2(np.random.permutation(np.resize(levels, k // 32))).repeat(32)
    a = np.empty((k // 512, 16))
    for p in range(k // 512):
        a[p, :8] = np.random.permutation(np.resize(levels, 8))
        for g in range(8):
            far = levels[np.abs(levels - a[p, g]) >= 10]
            a[p, g + 8] = far[np.random.randint(len(far))]
    return np.exp2(a.ravel()).repeat(32)


def f64(x):
    return np.asarray(x).astype(np.float64)


def striped(idx):
    return np.tile(idx.reshape(-1, 16).T, (8, 1)).astype(np.uint16)


def unstriped(offs):
    return offs[:16].T.reshape(-1).astype(np.int64)


E2M1 = np.array([0.0, 0.5, 1.0, 1.5, 2.0, 3.0, 4.0, 6.0, -0.0, -0.5, -1.0, -1.5, -2.0, -3.0, -4.0, -6.0])


def pack_weight(w, fmt):
    k, n = w.shape
    w = f64(np.asarray(w, np.float32).astype(ml_dtypes.bfloat16)).reshape(k // 32, 32, n)
    amax = np.abs(w).max(1)
    if fmt == "e4m3":
        byte = np.frexp(amax)[1] - 1 + 127 - 7
    else:
        mant, ex = np.frexp(amax / 6.0)
        byte = np.where(mant > 0.5, ex, ex - 1) + 127
    byte = np.clip(np.where(amax > 0, byte, 1), 1, 254)
    scaled = (w * np.exp2(127.0 - byte)[:, None, :]).reshape(k, n).astype(np.float32)
    by_word = np.ascontiguousarray(scaled.reshape(k // 512, 128, 4, n).transpose(0, 1, 3, 2))
    if fmt == "e4m3":
        words = by_word.astype(ml_dtypes.float8_e4m3fn).view(np.uint8)
    else:
        c = by_word.astype(ml_dtypes.float4_e2m1fn).view(np.uint8) & 0xF
        words = (c[..., 0::2] | (c[..., 1::2] << 4)).reshape(k // 512, 128, 2 * n)
    return np.ascontiguousarray(words), np.ascontiguousarray(byte.astype(np.uint8).reshape(k // 512, 16, n))


def unpack_weight(words, scales, fmt):
    g, _, n = scales.shape
    words = np.ascontiguousarray(words).reshape(g, 128, n, -1)
    if fmt == "e4m3":
        vals = words.view(ml_dtypes.float8_e4m3fn).astype(np.float64)
    else:
        nib = np.empty((g, 128, n, 4), np.uint8)
        nib[..., 0::2] = words & 0xF
        nib[..., 1::2] = words >> 4
        vals = E2M1[nib]
    vals = vals * np.repeat(np.exp2(scales.astype(np.float64) - 127.0), 8, axis=1)[..., None]
    return vals.transpose(0, 1, 3, 2).reshape(g * 512, n)


def gelu(v):
    return 0.5 * v * (1.0 + np.tanh(np.sqrt(2.0 / np.pi) * (v + 0.044715 * v**3)))


K, H, N, T, S, P = 1024, 1024, 384, 2048, 1024, 512


def setup_inputs():
    n = np.random.standard_normal
    s = mx_kscale(K)[:, None]
    u = mx_kscale(H)[:, None]
    tab_words, tab_scales = pack_weight(n((K, T)) * s, "e4m3")
    w2_words, w2_scales = pack_weight(0.95 * n((K, H)) / np.sqrt(K) / s, "e2m1")
    w4_words, w4_scales = pack_weight(n((H, N)) / np.sqrt(H) / u, "e4m3")
    return {
        "tab_words": tab_words,
        "tab_scales": tab_scales,
        "offs": striped(np.random.permutation(T)[:S]),
        "pos1": striped(np.random.permutation(S)[:P]),
        "pos2": striped(np.random.permutation(S)[:P]),
        "w1": (n((K, H)) / np.sqrt(K) / s).astype(np.float32),
        "w2_words": w2_words,
        "w2_scales": w2_scales,
        "w3": (1.8 * n((H, N)) / np.sqrt(H) / u).astype(np.float32),
        "w4_words": w4_words,
        "w4_scales": w4_scales,
        "gam": np.random.uniform(0.2, 1.2, H).astype(np.float32),
        "slope": np.random.uniform(0.6, 3.0, H).astype(np.float32),
        "bias": n(H).astype(np.float32),
        "temp": np.random.uniform(0.4, 1.6, H).astype(np.float32),
        "sv": (n(H) * u[:, 0]).astype(np.float32),
        "mat": (n((H, P)) * u).astype(np.float32),
    }


def reference(tab_words, tab_scales, offs, pos1, pos2, w1, w2_words, w2_scales, w3,
              w4_words, w4_scales, gam, slope, bias, temp, sv, mat):
    v = unpack_weight(tab_words, tab_scales, "e4m3")[:, unstriped(offs)]
    h = mxq(f64(w1), 0, "e4m3").T @ v
    g = f64(gam)[:, None] * (unpack_weight(w2_words, w2_scales, "e2m1").T @ v)
    a = 1.0 / (1.0 + np.exp(-(f64(slope)[:, None] * h[:, unstriped(pos1)] + f64(bias)[:, None])))
    top = g.max(axis=1)
    c = np.exp(f64(temp)[:, None] * (g[:, unstriped(pos2)] - top[:, None]))
    y1 = mxq(f64(sv)[:, None] * np.maximum(a, c), 0, "e4m3")
    y2 = mxq(f64(mat) * a, 0, "e4m3")
    first = mxq(f64(w3), 0, "e4m3").T @ y1
    second = unpack_weight(w4_words, w4_scales, "e4m3").T @ y2
    return np.tanh(first) + second

@@ -1,0 +1,310 @@
+from contextlib import ExitStack
+
+import concourse.mybir as mybir
+
+K, H, N, T, S, PICK = 1024, 1024, 384, 2048, 1024, 512
+FLOPS = 2 * (2 * K * H * S + 2 * H * N * PICK)
+
+F32 = mybir.dt.float32
+BF16 = mybir.dt.bfloat16
+I32 = mybir.dt.int32
+U32 = mybir.dt.uint32
+U16 = mybir.dt.uint16
+U8 = mybir.dt.uint8
+E4M3 = mybir.dt.float8_e4m3fn_x4
+E2M1 = mybir.dt.float4_e2m1fn_x4
+ALU = mybir.AluOpType
+ACT = mybir.ActivationFunctionType
+
+P = 128
+PACK = 4
+KP = P * PACK
+BANK = 512
+HALF = PICK // 2
+LIVE = 24
+
+
+def tile_list_evacuation_drill_reading_kernel(
+    tc, tab_words, tab_scales, offs, pos1, pos2, w1, w2_words, w2_scales, w3,
+    w4_words, w4_scales, gam, slope, bias, temp, sv, mat, out,
+):
+    nc = tc.nc
+    with ExitStack() as ctx:
+        keep = ctx.enter_context(tc.tile_pool(name="keep", bufs=1))
+        wins = ctx.enter_context(tc.tile_pool(name="wins", bufs=1))
+        reuse = ctx.enter_context(tc.tile_pool(name="reuse", bufs=1))
+        hs = ctx.enter_context(tc.tile_pool(name="hs", bufs=1))
+        ring = ctx.enter_context(tc.tile_pool(name="ring", bufs=4))
+        psum = ctx.enter_context(tc.psum_pool(name="psum", bufs=8))
+
+        def rows_vector(engine, vec, name):
+            tile = keep.tile([P, 2 * PACK], F32, name=name)
+            engine.dma_start(
+                out=tile[:].rearrange("p (b i) -> p b i", b=2),
+                in_=vec.rearrange("(b p i) -> p b i", b=2, i=PACK),
+            )
+            return tile
+
+        offs_t = keep.tile([P, S // 16], U16, name="offs_t")
+        nc.sync.dma_start(offs_t[:], offs)
+        ts = reuse.tile([P, T], U8, name="ts", offset=23552)
+        for q in range(4):
+            nc.sync.dma_start(
+                out=ts[32 * q + LIVE : 32 * q + 32, :].bitcast(I32),
+                in_=tab_scales[:, 4 * q : 4 * q + 4, :].bitcast(I32),
+            )
+        w2sraw = reuse.tile([P, 2, H], U8, name="w2sraw", offset=45056)
+        nc.vector.memset(w2sraw[:].bitcast(I32), 0)
+        for q in range(4):
+            nc.vector.memset(ts[32 * q : 32 * q + LIVE, :].bitcast(I32), 0)
+        tw = [reuse.tile([P, T], U32, name="tw%d" % a, offset=4 * T * a, align_bytes=64) for a in range(2)]
+
+        def load_words(a):
+            nc.sync.dma_start(
+                out=tw[a][:].bitcast(I32),
+                in_=tab_words[a].rearrange("p t i -> p (t i)").bitcast(I32),
+            )
+
+        load_words(0)
+        w2raw = reuse.tile([P, 2, 2 * H], U8, name="w2raw", offset=36864)
+        nc.sync.dma_start(
+            out=w2raw[:].bitcast(I32),
+            in_=w2_words.rearrange("a p e -> p a e").bitcast(I32),
+        )
+        for q in range(4):
+            nc.sync.dma_start(
+                out=w2sraw[32 * q : 32 * q + 4, :, :].bitcast(I32),
+                in_=w2_scales[:, 4 * q : 4 * q + 4, :].rearrange("a r e -> r a e").bitcast(I32),
+            )
+        load_words(1)
+        pos2_t = keep.tile([P, PICK // 16], U16, name="pos2_t")
+        nc.sync.dma_start(pos2_t[:], pos2)
+        pos1_t = keep.tile([P, PICK // 16], U16, name="pos1_t")
+        nc.sync.dma_start(pos1_t[:], pos1)
+        gam_t = rows_vector(nc.gpsimd, gam, "gam_t")
+        temp_t = rows_vector(nc.gpsimd, temp, "temp_t")
+        slope_t = rows_vector(nc.gpsimd, slope, "slope_t")
+        bias_t = rows_vector(nc.gpsimd, bias, "bias_t")
+        sv_t = rows_vector(nc.gpsimd, sv, "sv_t")
+        w4s = keep.tile([P, 2, N], U8, name="w4s", align_bytes=64)
+        nc.gpsimd.memset(w4s[:].bitcast(I32), 0)
+        for q in range(4):
+            nc.gpsimd.dma_start(
+                out=w4s[32 * q : 32 * q + 4, :, :].bitcast(I32),
+                in_=w4_scales[:, 4 * q : 4 * q + 4, :].rearrange("a r e -> r a e").bitcast(I32),
+            )
+
+        gs = keep.tile([P, S], U8, name="gs", align_bytes=64)
+        nc.vector.tensor_copy(gs[:], ts[:].indirect(offs_t[:]))
+        vs = [keep.tile([P, S], U8, name="vs%d" % a, align_bytes=64) for a in range(2)]
+        for a in range(2):
+            nc.vector.memset(vs[a][96:128, :].bitcast(I32), 0)
+            nc.sync.dma_start(
+                out=vs[a][0:100, :].bitcast(I32),
+                in_=gs[LIVE + 4 * a : LIVE + 4 * a + 100, :].bitcast(I32),
+            )
+        vw = [keep.tile([P, S], U32, name="vw%d" % a, align_bytes=64) for a in range(2)]
+        w2s = [keep.tile([P, 2, KP], U8, name="w2s%d" % b, align_bytes=64) for b in range(2)]
+
+        def deal_w2_scales(b):
+            nc.vector.tensor_copy(
+                out=w2s[b][:].rearrange("p a (t m i) -> p a m t i", t=PACK, i=16),
+                in_=w2sraw[:, :, KP * b : KP * (b + 1)].rearrange("p a (m i t) -> p a m t i", t=PACK, i=16),
+            )
+
+        nc.vector.tensor_copy(vw[0][:], tw[0][:].indirect(offs_t[:]))
+        deal_w2_scales(0)
+        for n in range(2):
+            nc.vector.tensor_copy(
+                vw[1][:, BANK * n : BANK * (n + 1)], tw[1][:].indirect(offs_t[:, 32 * n : 32 * (n + 1)])
+            )
+        deal_w2_scales(1)
+
+        w2c = {}
+        for b in range(2):
+            for a in range(2):
+                w2c[a, b] = keep.tile([P, 2 * KP], U8, name="w2c%d%d" % (a, b), align_bytes=64)
+                nc.scalar.copy(
+                    out=w2c[a, b][:].bitcast(U16).rearrange("p (t m i) -> p m t i", t=PACK, i=8),
+                    in_=w2raw[:, a, 2 * KP * b : 2 * KP * (b + 1)].bitcast(U16).rearrange(
+                        "p (m i t) -> p m t i", t=PACK, i=8
+                    ),
+                )
+
+        def load_rows(src, name, offset):
+            tile = reuse.tile([P, PACK, src.shape[1]], F32, name=name, offset=offset)
+            nc.sync.dma_start(out=tile[:], in_=src.rearrange("(p j) c -> p j c", j=PACK))
+            return tile
+
+        w1raw = {}
+        for (a, b), offset in (((0, 0), 16384), ((1, 0), 24576), ((0, 1), 0), ((1, 1), 36864)):
+            w1raw[a, b] = load_rows(w1[KP * a : KP * (a + 1), KP * b : KP * (b + 1)], "w1raw%d%d" % (a, b), offset)
+        w4c = reuse.tile([P, 2, N], U32, name="w4c", offset=45056)
+        nc.sync.dma_start(
+            out=w4c[:].bitcast(I32),
+            in_=w4_words.rearrange("a p e i -> p a (e i)").bitcast(I32),
+        )
+        ntemp = keep.tile([P, 2 * PACK], F32, name="ntemp")
+        nc.gpsimd.tensor_scalar(out=ntemp[:], in0=temp_t[:], scalar1=-1.0, scalar2=0.0, op0=ALU.mult, op1=ALU.add)
+
+        def first_stage(codes, scales, n):
+            bank = psum.tile([P, BANK], F32, name="bank", tag="bank")
+            cols = slice(BANK * n, BANK * (n + 1))
+            for a in range(2):
+                nc.tensor.matmul_mx(
+                    out=bank[:], lhsT=codes[a], lhsT_scale=scales[a],
+                    rhs=vw[a][:, cols].bitcast(E4M3), rhs_scale=vs[a][:, cols],
+                    start=(a == 0), stop=(a == 1),
+                )
+            return bank
+
+        tops = keep.tile([P, 16], F32, name="tops")
+        ebias = keep.tile([P, 8], F32, name="ebias")
+        c_t = [keep.tile([P, PACK, PICK], F32, name="c%d" % b) for b in range(2)]
+
+        def g_tile(j):
+            b, t = divmod(j, PACK)
+            g = wins.tile([P, S], F32, name="g%d" % j, offset=4 * S * j)
+            for n in range(2):
+                bank = first_stage(
+                    [w2c[a, b][:, 2 * P * t : 2 * P * (t + 1)].bitcast(E2M1) for a in range(2)],
+                    [w2s[b][:, a, P * t : P * (t + 1)] for a in range(2)], n,
+                )
+                nc.vector.tensor_scalar(
+                    out=g[:, BANK * n : BANK * (n + 1)], in0=bank[:], scalar1=gam_t[:, j : j + 1], scalar2=None,
+                    op0=ALU.mult, op1=ALU.max, accum_out=tops[:, 2 * j + n : 2 * j + n + 1],
+                )
+            nc.gpsimd.tensor_scalar(
+                out=ebias[:, j : j + 1], in0=tops[:, 2 * j : 2 * j + 1], scalar1=tops[:, 2 * j + 1 : 2 * j + 2],
+                scalar2=ntemp[:, j : j + 1], op0=ALU.max, op1=ALU.mult,
+            )
+            nc.scalar.activation(
+                out=c_t[b][:, t, :], in_=g[:].indirect(pos2_t[:]), func=ACT.Exp,
+                bias=ebias[:, j : j + 1], scale=temp_t[:, j : j + 1],
+            )
+
+        w1c, w1s = {}, {}
+
+        def quantise_w1(a, b, copy):
+            grouped = ring.tile([P, PACK * KP], BF16, name="grouped", tag="grouped", align_bytes=64)
+            copy(grouped, w1raw[a, b])
+            w1c[a, b] = keep.tile([P, KP], U32, name="w1c%d%d" % (a, b), align_bytes=64)
+            w1s[a, b] = keep.tile([P, KP], U8, name="w1s%d%d" % (a, b), align_bytes=64)
+            nc.vector.quantize_mx(out=w1c[a, b][:].bitcast(E4M3), scales=w1s[a, b][:], in_=grouped[:])
+
+        def paired(copy):
+            return lambda grouped, raw: copy(
+                out=grouped[:].rearrange("p (u v m j) -> p m u j v", u=2, v=2, j=PACK),
+                in_=raw[:].rearrange("p j (m u v) -> p m u j v", u=2, v=2),
+            )
+
+        def pool_cast(grouped, raw):
+            nc.gpsimd.tensor_copy(
+                out=grouped[:].rearrange("p (t m j) -> p m t j", t=PACK, j=PACK),
+                in_=raw[:].rearrange("p j (m t) -> p m t j", t=PACK),
+            )
+
+        casts = {"scalar": paired(nc.scalar.copy), "vector": paired(nc.vector.tensor_copy), "gpsimd": pool_cast}
+        h_t = {}
+
+        def h_tile(j, copy):
+            b, t = divmod(j, PACK)
+            h_t[j] = hs.tile([P, S], F32, name="h%d" % j, offset=4 * S * j)
+            for n in range(2):
+                bank = first_stage(
+                    [w1c[a, b][:, P * t : P * (t + 1)].bitcast(E4M3) for a in range(2)],
+                    [w1s[a, b][:, P * t : P * (t + 1)] for a in range(2)], n,
+                )
+                copy(out=h_t[j][:, BANK * n : BANK * (n + 1)], in_=bank[:])
+
+        for j in range(4):
+            g_tile(j)
+        quantise_w1(0, 0, casts["scalar"])
+        quantise_w1(1, 0, casts["scalar"])
+        mat_t = [load_rows(mat[0:KP, :], "mat0", 8192)]
+        w3raw = [load_rows(w3[KP * b : KP * (b + 1), :], "w3raw%d" % b, 16384 + 6144 * b) for b in range(2)]
+        mat_t.append(load_rows(mat[KP : 2 * KP, :], "mat1", 28672))
+        for j in range(4, 8):
+            g_tile(j)
+        for j in range(4):
+            h_tile(j, nc.vector.tensor_copy if j < 4 else nc.scalar.copy)
+        quantise_w1(0, 1, casts["vector"])
+        quantise_w1(1, 1, casts["vector"])
+
+        a_t = [
+            wins.tile([P, PACK, PICK], F32, name="a%d" % b, offset=4 * S * 7 + 2048 - 8192 * (1 - b)) for b in range(2)
+        ]
+        yc, ysc = {}, {}
+        WALK = 2
+
+        def looks(b, u):
+            for t in range(PACK):
+                j = PACK * b + t
+                nc.scalar.activation(
+                    out=a_t[b][:, t, HALF * u : HALF * (u + 1)], in_=h_t[j][:].indirect(pos1_t[:, 16 * u : 16 * (u + 1)]),
+                    func=ACT.Sigmoid, bias=bias_t[:, j : j + 1], scale=slope_t[:, j : j + 1],
+                )
+
+        def signals(b, u):
+            cols = slice(HALF * u, HALF * (u + 1))
+            ys = ring.tile([P, 2, PACK * HALF], BF16, name="ys", tag="grouped", align_bytes=64)
+            walk = "p t (c i) -> p c t i"
+            yc[b, u] = keep.tile([P, 2, HALF], U32, name="yc%d%d" % (b, u), align_bytes=64)
+            ysc[b, u] = keep.tile([P, 2, HALF], U8, name="ysc%d%d" % (b, u), align_bytes=64)
+            nc.vector.tensor_tensor(
+                out=ys[:, 1, :].rearrange("p (c i t) -> p c t i", i=WALK, t=PACK),
+                in0=a_t[b][:, :, cols].rearrange(walk, i=WALK), in1=mat_t[b][:, :, cols].rearrange(walk, i=WALK),
+                op=ALU.mult,
+            )
+            nc.vector.tensor_tensor(out=c_t[b][:, :, cols], in0=a_t[b][:, :, cols], in1=c_t[b][:, :, cols], op=ALU.max)
+            nc.vector.quantize_mx(out=yc[b, u][:, 1, :].bitcast(E4M3), scales=ysc[b, u][:, 1, :], in_=ys[:, 1, :])
+            nc.vector.tensor_tensor(
+                out=ys[:, 0, :].rearrange("p (c i t) -> p c t i", i=WALK, t=PACK),
+                in0=c_t[b][:, :, cols].rearrange(walk, i=WALK),
+                in1=sv_t[:, PACK * b : PACK * (b + 1)].unsqueeze(1).unsqueeze(3).to_broadcast([P, HALF // WALK, PACK, WALK]),
+                op=ALU.mult,
+            )
+            nc.vector.quantize_mx(out=yc[b, u][:, 0, :].bitcast(E4M3), scales=ysc[b, u][:, 0, :], in_=ys[:, 0, :])
+
+        for u in range(2):
+            looks(0, u)
+            signals(0, u)
+        for j in range(4, 8):
+            h_tile(j, nc.scalar.copy)
+        for u in range(2):
+            looks(1, u)
+        signals(1, 0)
+
+        w3c, w3s = [], []
+        for b in range(2):
+            grouped3 = hs.tile([P, PACK * N], BF16, name="grouped3%d" % b, offset=4 * S * (6 + b), align_bytes=64)
+            nc.scalar.copy(
+                out=grouped3[:].rearrange("p (c i j) -> p c j i", i=WALK, j=PACK),
+                in_=w3raw[b][:].rearrange("p j (c i) -> p c j i", i=WALK),
+            )
+            w3c.append(keep.tile([P, N], U32, name="w3c%d" % b, align_bytes=64))
+            w3s.append(keep.tile([P, N], U8, name="w3s%d" % b, align_bytes=64))
+            nc.vector.quantize_mx(out=w3c[b][:].bitcast(E4M3), scales=w3s[b][:], in_=grouped3[:])
+        signals(1, 1)
+
+        for u in range(2):
+            result = [psum.tile([P, BANK], F32, name="res%d%d" % (u, k), tag="bank") for k in range(3)]
+            for b in range(2):
+                for k in range(3):
+                    rows = slice(P * k, P * (k + 1))
+                    nc.tensor.matmul_mx(
+                        out=result[k][:, HALF:BANK], lhsT=w4c[:, b, rows].bitcast(E4M3), lhsT_scale=w4s[:, b, rows],
+                        rhs=yc[b, u][:, 1, :].bitcast(E4M3), rhs_scale=ysc[b, u][:, 1, :], start=(b == 0), stop=False,
+                    )
+            for b in range(2):
+                for k in range(3):
+                    rows = slice(P * k, P * (k + 1))
+                    nc.tensor.matmul_mx(
+                        out=result[k][:, 0:HALF], lhsT=w3c[b][:, rows].bitcast(E4M3), lhsT_scale=w3s[b][:, rows],
+                        rhs=yc[b, u][:, 0, :].bitcast(E4M3), rhs_scale=ysc[b, u][:, 0, :], start=False, stop=(b == 1),
+                    )
+            for k in range(3):
+                bounded = keep.tile([P, HALF], F32, name="bounded%d%d" % (u, k))
+                nc.scalar.activation(out=bounded[:], in_=result[k][:, 0:HALF], func=ACT.Tanh)
+                nc.vector.tensor_tensor(out=bounded[:], in0=result[k][:, HALF:BANK], in1=bounded[:], op=ALU.add)
+                nc.sync.dma_start(out=out[P * k : P * (k + 1), HALF * u : HALF * (u + 1)], in_=bounded[:])

@@ -21,7 +21,29 @@ PACK = 4
 KP = P * PACK
 BANK = 512
 HALF = PICK // 2
+PER_COLUMN = 16
 LIVE = 24
+MOVED = 100
+KB = 1024
+
+AT_TAB_WORDS = [0, 8 * KB]
+AT_TAB_SCALES = 27 * KB
+AT_W2_WORDS = 44 * KB
+AT_W2_SCALES = 52 * KB
+AT_PICKED_SCALES = 54 * KB
+AT_W1 = {(0, 0): 20 * KB, (1, 0): 28 * KB, (0, 1): AT_TAB_WORDS[0], (1, 1): AT_TAB_WORDS[1]}
+AT_W3 = [40 * KB, 46 * KB]
+AT_W4_SCALES = AT_PICKED_SCALES
+AT_W4_WORDS = AT_W1[0, 1]
+AT_C0 = 16 * KB
+AT_MAT = [24 * KB, 32 * KB]
+AT_G = [4 * KB * j for j in range(7)] + [34 * KB]
+AT_A = [28 * KB, 36 * KB]
+AT_H = [44 * KB + 4 * KB * j for j in range(3)] + [58 * KB, 56 * KB, 60 * KB, 64 * KB, 68 * KB]
+AT_EARLY = 0
+AT_LATE = 8 * KB
+AT_W1_CODES = [AT_LATE, 16 * KB]
+AT_W2_DEALT = [20 * KB, AT_LATE]
 
 
 def tile_list_evacuation_drill_reading_kernel(
@@ -31,121 +53,117 @@ def tile_list_evacuation_drill_reading_kernel(
     nc = tc.nc
     with ExitStack() as ctx:
         keep = ctx.enter_context(tc.tile_pool(name="keep", bufs=1))
-        wins = ctx.enter_context(tc.tile_pool(name="wins", bufs=1))
-        reuse = ctx.enter_context(tc.tile_pool(name="reuse", bufs=1))
-        hs = ctx.enter_context(tc.tile_pool(name="hs", bufs=1))
-        ring = ctx.enter_context(tc.tile_pool(name="ring", bufs=4))
+        rows = ctx.enter_context(tc.tile_pool(name="rows", bufs=1))
+        loads = ctx.enter_context(tc.tile_pool(name="loads", bufs=1))
+        stage = ctx.enter_context(tc.tile_pool(name="stage", bufs=1))
         psum = ctx.enter_context(tc.psum_pool(name="psum", bufs=8))
 
-        def rows_vector(engine, vec, name):
+        def load_list(src, name):
+            tile = keep.tile(list(src.shape), U16, name=name)
+            nc.sync.dma_start(tile[:], src)
+            return tile
+
+        def load_per_row(vec, name):
             tile = keep.tile([P, 2 * PACK], F32, name=name)
-            engine.dma_start(
-                out=tile[:].rearrange("p (b i) -> p b i", b=2),
-                in_=vec.rearrange("(b p i) -> p b i", b=2, i=PACK),
+            nc.gpsimd.dma_start(
+                out=tile[:].rearrange("p (b t) -> p b t", b=2), in_=vec.rearrange("(b p t) -> p b t", b=2, t=PACK)
             )
             return tile
 
-        offs_t = keep.tile([P, S // 16], U16, name="offs_t")
-        nc.sync.dma_start(offs_t[:], offs)
-        ts = reuse.tile([P, T], U8, name="ts", offset=23552)
+        def load_scales(tile, src):
+            for q in range(4):
+                nc.sync.dma_start(
+                    out=tile[32 * q : 32 * q + 4, :, :].bitcast(I32),
+                    in_=src[:, 4 * q : 4 * q + 4, :].rearrange("a s e -> s a e").bitcast(I32),
+                )
+
+        def load_pass(src, name, offset):
+            tile = loads.tile([P, PACK, src.shape[1]], F32, name=name, offset=offset)
+            nc.sync.dma_start(out=tile[:], in_=src.rearrange("(p i) c -> p i c", i=PACK))
+            return tile
+
+        offs_t = load_list(offs, "offs_t")
+        tab_s = loads.tile([P, T], U8, name="tab_s", offset=AT_TAB_SCALES)
         for q in range(4):
             nc.sync.dma_start(
-                out=ts[32 * q + LIVE : 32 * q + 32, :].bitcast(I32),
+                out=tab_s[32 * q + LIVE : 32 * q + 32, :].bitcast(I32),
                 in_=tab_scales[:, 4 * q : 4 * q + 4, :].bitcast(I32),
             )
-        w2sraw = reuse.tile([P, 2, H], U8, name="w2sraw", offset=45056)
-        nc.vector.memset(w2sraw[:].bitcast(I32), 0)
+        w2_s = loads.tile([P, 2, H], U8, name="w2_s", offset=AT_W2_SCALES)
+        nc.gpsimd.memset(w2_s[:].bitcast(I32), 0)
         for q in range(4):
-            nc.vector.memset(ts[32 * q : 32 * q + LIVE, :].bitcast(I32), 0)
-        tw = [reuse.tile([P, T], U32, name="tw%d" % a, offset=4 * T * a, align_bytes=64) for a in range(2)]
+            engine = nc.vector if q < 3 else nc.gpsimd
+            engine.memset(tab_s[32 * q : 32 * q + LIVE, :].bitcast(I32), 0)
+        v_scales = [keep.tile([P, S], U8, name="v_scales%d" % a, align_bytes=64) for a in range(2)]
+        for a in range(2):
+            nc.gpsimd.memset(v_scales[a][96:P, :].bitcast(I32), 0)
+        tab_w = [loads.tile([P, T], U32, name="tab_w%d" % a, offset=AT_TAB_WORDS[a], align_bytes=64) for a in range(2)]
 
         def load_words(a):
             nc.sync.dma_start(
-                out=tw[a][:].bitcast(I32),
-                in_=tab_words[a].rearrange("p t i -> p (t i)").bitcast(I32),
+                out=tab_w[a][:].bitcast(I32), in_=tab_words[a].rearrange("p t i -> p (t i)").bitcast(I32)
             )
 
         load_words(0)
-        w2raw = reuse.tile([P, 2, 2 * H], U8, name="w2raw", offset=36864)
-        nc.sync.dma_start(
-            out=w2raw[:].bitcast(I32),
-            in_=w2_words.rearrange("a p e -> p a e").bitcast(I32),
-        )
-        for q in range(4):
-            nc.sync.dma_start(
-                out=w2sraw[32 * q : 32 * q + 4, :, :].bitcast(I32),
-                in_=w2_scales[:, 4 * q : 4 * q + 4, :].rearrange("a r e -> r a e").bitcast(I32),
-            )
+        load_scales(w2_s, w2_scales)
         load_words(1)
-        pos2_t = keep.tile([P, PICK // 16], U16, name="pos2_t")
-        nc.sync.dma_start(pos2_t[:], pos2)
-        pos1_t = keep.tile([P, PICK // 16], U16, name="pos1_t")
-        nc.sync.dma_start(pos1_t[:], pos1)
-        gam_t = rows_vector(nc.gpsimd, gam, "gam_t")
-        temp_t = rows_vector(nc.gpsimd, temp, "temp_t")
-        slope_t = rows_vector(nc.gpsimd, slope, "slope_t")
-        bias_t = rows_vector(nc.gpsimd, bias, "bias_t")
-        sv_t = rows_vector(nc.gpsimd, sv, "sv_t")
-        w4s = keep.tile([P, 2, N], U8, name="w4s", align_bytes=64)
-        nc.gpsimd.memset(w4s[:].bitcast(I32), 0)
-        for q in range(4):
-            nc.gpsimd.dma_start(
-                out=w4s[32 * q : 32 * q + 4, :, :].bitcast(I32),
-                in_=w4_scales[:, 4 * q : 4 * q + 4, :].rearrange("a r e -> r a e").bitcast(I32),
-            )
+        w2_w = loads.tile([P, 2, 2 * H], U8, name="w2_w", offset=AT_W2_WORDS)
+        nc.sync.dma_start(out=w2_w[:].bitcast(I32), in_=w2_words.rearrange("a p e -> p a e").bitcast(I32))
+        pos2_t = load_list(pos2, "pos2_t")
+        pos1_t = load_list(pos1, "pos1_t")
+        gam_t = load_per_row(gam, "gam_t")
+        temp_t = load_per_row(temp, "temp_t")
+        slope_t = load_per_row(slope, "slope_t")
+        bias_t = load_per_row(bias, "bias_t")
+        sv_t = load_per_row(sv, "sv_t")
 
-        gs = keep.tile([P, S], U8, name="gs", align_bytes=64)
-        nc.vector.tensor_copy(gs[:], ts[:].indirect(offs_t[:]))
-        vs = [keep.tile([P, S], U8, name="vs%d" % a, align_bytes=64) for a in range(2)]
+        picked_s = loads.tile([P, S], U8, name="picked_s", offset=AT_PICKED_SCALES)
+        nc.vector.tensor_copy(picked_s[:], tab_s[:].indirect(offs_t[:]))
         for a in range(2):
-            nc.vector.memset(vs[a][96:128, :].bitcast(I32), 0)
+            first = LIVE + 4 * a
             nc.sync.dma_start(
-                out=vs[a][0:100, :].bitcast(I32),
-                in_=gs[LIVE + 4 * a : LIVE + 4 * a + 100, :].bitcast(I32),
+                out=v_scales[a][0:MOVED, :].bitcast(I32), in_=picked_s[first : first + MOVED, :].bitcast(I32)
             )
-        vw = [keep.tile([P, S], U32, name="vw%d" % a, align_bytes=64) for a in range(2)]
-        w2s = [keep.tile([P, 2, KP], U8, name="w2s%d" % b, align_bytes=64) for b in range(2)]
+        v_words = [keep.tile([P, S], U32, name="v_words%d" % a, align_bytes=64) for a in range(2)]
+        w2_scale = [keep.tile([P, 2, KP], U8, name="w2_scale%d" % b, align_bytes=64) for b in range(2)]
 
         def deal_w2_scales(b):
             nc.vector.tensor_copy(
-                out=w2s[b][:].rearrange("p a (t m i) -> p a m t i", t=PACK, i=16),
-                in_=w2sraw[:, :, KP * b : KP * (b + 1)].rearrange("p a (m i t) -> p a m t i", t=PACK, i=16),
+                out=w2_scale[b][:].rearrange("p a (t m i) -> p a m t i", t=PACK, i=16),
+                in_=w2_s[:, :, KP * b : KP * (b + 1)].rearrange("p a (m i t) -> p a m t i", t=PACK, i=16),
             )
 
-        nc.vector.tensor_copy(vw[0][:], tw[0][:].indirect(offs_t[:]))
+        nc.vector.tensor_copy(v_words[0][:], tab_w[0][:].indirect(offs_t[:]))
         deal_w2_scales(0)
         for n in range(2):
-            nc.vector.tensor_copy(
-                vw[1][:, BANK * n : BANK * (n + 1)], tw[1][:].indirect(offs_t[:, 32 * n : 32 * (n + 1)])
-            )
+            entries = slice(BANK * n // PER_COLUMN, BANK * (n + 1) // PER_COLUMN)
+            nc.vector.tensor_copy(v_words[1][:, BANK * n : BANK * (n + 1)], tab_w[1][:].indirect(offs_t[:, entries]))
         deal_w2_scales(1)
 
-        w2c = {}
+        w2_code = {}
         for b in range(2):
             for a in range(2):
-                w2c[a, b] = keep.tile([P, 2 * KP], U8, name="w2c%d%d" % (a, b), align_bytes=64)
+                w2_code[a, b] = stage.tile(
+                    [P, 2 * KP], U8, name="w2_code%d%d" % (a, b), offset=AT_W2_DEALT[b] + KB * a, align_bytes=64
+                )
                 nc.scalar.copy(
-                    out=w2c[a, b][:].bitcast(U16).rearrange("p (t m i) -> p m t i", t=PACK, i=8),
-                    in_=w2raw[:, a, 2 * KP * b : 2 * KP * (b + 1)].bitcast(U16).rearrange(
+                    out=w2_code[a, b][:].bitcast(U16).rearrange("p (t m i) -> p m t i", t=PACK, i=8),
+                    in_=w2_w[:, a, 2 * KP * b : 2 * KP * (b + 1)].bitcast(U16).rearrange(
                         "p (m i t) -> p m t i", t=PACK, i=8
                     ),
                 )
 
-        def load_rows(src, name, offset):
-            tile = reuse.tile([P, PACK, src.shape[1]], F32, name=name, offset=offset)
-            nc.sync.dma_start(out=tile[:], in_=src.rearrange("(p j) c -> p j c", j=PACK))
-            return tile
-
-        w1raw = {}
-        for (a, b), offset in (((0, 0), 16384), ((1, 0), 24576), ((0, 1), 0), ((1, 1), 36864)):
-            w1raw[a, b] = load_rows(w1[KP * a : KP * (a + 1), KP * b : KP * (b + 1)], "w1raw%d%d" % (a, b), offset)
-        w4c = reuse.tile([P, 2, N], U32, name="w4c", offset=45056)
-        nc.sync.dma_start(
-            out=w4c[:].bitcast(I32),
-            in_=w4_words.rearrange("a p e i -> p a (e i)").bitcast(I32),
-        )
-        ntemp = keep.tile([P, 2 * PACK], F32, name="ntemp")
-        nc.gpsimd.tensor_scalar(out=ntemp[:], in0=temp_t[:], scalar1=-1.0, scalar2=0.0, op0=ALU.mult, op1=ALU.add)
+        w1_raw = {}
+        for b in range(2):
+            for a in range(2):
+                block = w1[KP * a : KP * (a + 1), KP * b : KP * (b + 1)]
+                w1_raw[a, b] = load_pass(block, "w1_raw%d%d" % (a, b), AT_W1[a, b])
+        w3_raw = [load_pass(w3[KP * b : KP * (b + 1), :], "w3_raw%d" % b, AT_W3[b]) for b in range(2)]
+        w4_scale = loads.tile([P, 2, N], U8, name="w4_scale", offset=AT_W4_SCALES)
+        nc.gpsimd.memset(w4_scale[:].bitcast(I32), 0)
+        load_scales(w4_scale, w4_scales)
+        minus_temp = keep.tile([P, 2 * PACK], F32, name="minus_temp")
+        nc.gpsimd.tensor_scalar(out=minus_temp[:], in0=temp_t[:], scalar1=-1.0, scalar2=0.0, op0=ALU.mult, op1=ALU.add)
 
         def first_stage(codes, scales, n):
             bank = psum.tile([P, BANK], F32, name="bank", tag="bank")
@@ -153,158 +171,205 @@ def tile_list_evacuation_drill_reading_kernel(
             for a in range(2):
                 nc.tensor.matmul_mx(
                     out=bank[:], lhsT=codes[a], lhsT_scale=scales[a],
-                    rhs=vw[a][:, cols].bitcast(E4M3), rhs_scale=vs[a][:, cols],
+                    rhs=v_words[a][:, cols].bitcast(E4M3), rhs_scale=v_scales[a][:, cols],
                     start=(a == 0), stop=(a == 1),
                 )
             return bank
 
-        tops = keep.tile([P, 16], F32, name="tops")
-        ebias = keep.tile([P, 8], F32, name="ebias")
-        c_t = [keep.tile([P, PACK, PICK], F32, name="c%d" % b) for b in range(2)]
+        bank_max = keep.tile([P, 2 * 2 * PACK], F32, name="bank_max")
+        exp_bias = keep.tile([P, 2 * PACK], F32, name="exp_bias")
+        c_t = [loads.tile([P, PACK, PICK], F32, name="c0", offset=AT_C0), keep.tile([P, PACK, PICK], F32, name="c1")]
 
         def g_tile(j):
             b, t = divmod(j, PACK)
-            g = wins.tile([P, S], F32, name="g%d" % j, offset=4 * S * j)
+            g = rows.tile([P, S], F32, name="g%d" % j, offset=AT_G[j])
             for n in range(2):
                 bank = first_stage(
-                    [w2c[a, b][:, 2 * P * t : 2 * P * (t + 1)].bitcast(E2M1) for a in range(2)],
-                    [w2s[b][:, a, P * t : P * (t + 1)] for a in range(2)], n,
+                    [w2_code[a, b][:, 2 * P * t : 2 * P * (t + 1)].bitcast(E2M1) for a in range(2)],
+                    [w2_scale[b][:, a, P * t : P * (t + 1)] for a in range(2)], n,
                 )
                 nc.vector.tensor_scalar(
                     out=g[:, BANK * n : BANK * (n + 1)], in0=bank[:], scalar1=gam_t[:, j : j + 1], scalar2=None,
-                    op0=ALU.mult, op1=ALU.max, accum_out=tops[:, 2 * j + n : 2 * j + n + 1],
+                    op0=ALU.mult, op1=ALU.max, accum_out=bank_max[:, 2 * j + n : 2 * j + n + 1],
                 )
             nc.gpsimd.tensor_scalar(
-                out=ebias[:, j : j + 1], in0=tops[:, 2 * j : 2 * j + 1], scalar1=tops[:, 2 * j + 1 : 2 * j + 2],
-                scalar2=ntemp[:, j : j + 1], op0=ALU.max, op1=ALU.mult,
+                out=exp_bias[:, j : j + 1], in0=bank_max[:, 2 * j : 2 * j + 1],
+                scalar1=bank_max[:, 2 * j + 1 : 2 * j + 2], scalar2=minus_temp[:, j : j + 1],
+                op0=ALU.max, op1=ALU.mult,
             )
             nc.scalar.activation(
                 out=c_t[b][:, t, :], in_=g[:].indirect(pos2_t[:]), func=ACT.Exp,
-                bias=ebias[:, j : j + 1], scale=temp_t[:, j : j + 1],
+                bias=exp_bias[:, j : j + 1], scale=temp_t[:, j : j + 1],
             )
 
-        w1c, w1s = {}, {}
+        def round_w1(b, copy):
+            rounded = stage.tile(
+                [P, 2, PACK * KP], BF16, name="w1_rounded%d" % b, offset=[AT_EARLY, AT_LATE][b], align_bytes=64
+            )
+            for a in range(2):
+                dst = rounded[:, a, :].rearrange("p (u v m i) -> p u m i v", u=2, v=2, i=PACK)
+                src = w1_raw[a, b][:].rearrange("p i (m u v) -> p u m i v", u=2, v=2)
+                for u in range(2):
+                    copy(out=dst[:, u], in_=src[:, u])
+            return rounded
 
-        def quantise_w1(a, b, copy):
-            grouped = ring.tile([P, PACK * KP], BF16, name="grouped", tag="grouped", align_bytes=64)
-            copy(grouped, w1raw[a, b])
-            w1c[a, b] = keep.tile([P, KP], U32, name="w1c%d%d" % (a, b), align_bytes=64)
-            w1s[a, b] = keep.tile([P, KP], U8, name="w1s%d%d" % (a, b), align_bytes=64)
-            nc.vector.quantize_mx(out=w1c[a, b][:].bitcast(E4M3), scales=w1s[a, b][:], in_=grouped[:])
+        w1_code, w1_scale = {}, {}
 
-        def paired(copy):
-            return lambda grouped, raw: copy(
-                out=grouped[:].rearrange("p (u v m j) -> p m u j v", u=2, v=2, j=PACK),
-                in_=raw[:].rearrange("p j (m u v) -> p m u j v", u=2, v=2),
+        def quantise_w1(b, rounded):
+            w1_code[b] = stage.tile([P, 2, KP], U32, name="w1_code%d" % b, offset=AT_W1_CODES[b], align_bytes=64)
+            w1_scale[b] = keep.tile([P, 2, KP], U8, name="w1_scale%d" % b, align_bytes=64)
+            nc.vector.quantize_mx(
+                out=w1_code[b][:].rearrange("p a c -> p (a c)").bitcast(E4M3),
+                scales=w1_scale[b][:].rearrange("p a c -> p (a c)"),
+                in_=rounded[:].rearrange("p a c -> p (a c)"),
             )
 
-        def pool_cast(grouped, raw):
-            nc.gpsimd.tensor_copy(
-                out=grouped[:].rearrange("p (t m j) -> p m t j", t=PACK, j=PACK),
-                in_=raw[:].rearrange("p j (m t) -> p m t j", t=PACK),
-            )
-
-        casts = {"scalar": paired(nc.scalar.copy), "vector": paired(nc.vector.tensor_copy), "gpsimd": pool_cast}
         h_t = {}
 
         def h_tile(j, copy):
             b, t = divmod(j, PACK)
-            h_t[j] = hs.tile([P, S], F32, name="h%d" % j, offset=4 * S * j)
+            h_t[j] = rows.tile([P, S], F32, name="h%d" % j, offset=AT_H[j])
             for n in range(2):
                 bank = first_stage(
-                    [w1c[a, b][:, P * t : P * (t + 1)].bitcast(E4M3) for a in range(2)],
-                    [w1s[a, b][:, P * t : P * (t + 1)] for a in range(2)], n,
+                    [w1_code[b][:, a, P * t : P * (t + 1)].bitcast(E4M3) for a in range(2)],
+                    [w1_scale[b][:, a, P * t : P * (t + 1)] for a in range(2)], n,
                 )
                 copy(out=h_t[j][:, BANK * n : BANK * (n + 1)], in_=bank[:])
 
-        for j in range(4):
+        w1_rounded = round_w1(0, nc.scalar.copy)
+        for j in range(PACK):
             g_tile(j)
-        quantise_w1(0, 0, casts["scalar"])
-        quantise_w1(1, 0, casts["scalar"])
-        mat_t = [load_rows(mat[0:KP, :], "mat0", 8192)]
-        w3raw = [load_rows(w3[KP * b : KP * (b + 1), :], "w3raw%d" % b, 16384 + 6144 * b) for b in range(2)]
-        mat_t.append(load_rows(mat[KP : 2 * KP, :], "mat1", 28672))
-        for j in range(4, 8):
+        mat_t = [load_pass(mat[KP * b : KP * (b + 1), :], "mat%d" % b, AT_MAT[b]) for b in range(2)]
+        for j in range(PACK, 2 * PACK):
             g_tile(j)
-        for j in range(4):
-            h_tile(j, nc.vector.tensor_copy if j < 4 else nc.scalar.copy)
-        quantise_w1(0, 1, casts["vector"])
-        quantise_w1(1, 1, casts["vector"])
+        quantise_w1(0, w1_rounded)
+        for j in range(PACK):
+            h_tile(j, nc.vector.tensor_copy)
+        quantise_w1(1, round_w1(1, nc.vector.tensor_copy))
+        w4_code = loads.tile([P, 2, N], U32, name="w4_code", offset=AT_W4_WORDS)
+        nc.sync.dma_start(out=w4_code[:].bitcast(I32), in_=w4_words.rearrange("a p e i -> p a (e i)").bitcast(I32))
 
-        a_t = [
-            wins.tile([P, PACK, PICK], F32, name="a%d" % b, offset=4 * S * 7 + 2048 - 8192 * (1 - b)) for b in range(2)
+        a_t = [rows.tile([P, PACK, PICK], F32, name="a%d" % b, offset=AT_A[b]) for b in range(2)]
+        y_code = [keep.tile([P, 2, PICK], U32, name="y_code%d" % b, align_bytes=64) for b in range(2)]
+        y_scale = [keep.tile([P, 2, PICK], U8, name="y_scale%d" % b, align_bytes=64) for b in range(2)]
+
+        def by_row_tile(ap, run):
+            return ap.rearrange("p t (c i) -> p c t i", i=run)
+
+        def by_word(ap, run):
+            return ap.rearrange("p (c i t) -> p c t i", i=run, t=PACK)
+
+        PAIR = 2
+
+        def look(b, t, cols):
+            j = PACK * b + t
+            entries = slice(cols.start // PER_COLUMN, cols.stop // PER_COLUMN)
+            nc.scalar.activation(
+                out=a_t[b][:, t, cols], in_=h_t[j][:].indirect(pos1_t[:, entries]), func=ACT.Sigmoid,
+                bias=bias_t[:, j : j + 1], scale=slope_t[:, j : j + 1],
+            )
+
+        def stronger(b, tiles, cols):
+            nc.vector.tensor_tensor(
+                out=c_t[b][:, tiles, cols], in0=a_t[b][:, tiles, cols], in1=c_t[b][:, tiles, cols], op=ALU.max
+            )
+
+        def make_y1(b, cols, y):
+            count = (cols.stop - cols.start) // PAIR
+            factor = sv_t[:, PACK * b : PACK * (b + 1)].unsqueeze(1).unsqueeze(3).to_broadcast([P, count, PACK, PAIR])
+            nc.vector.tensor_tensor(
+                out=by_word(y, PAIR), in0=by_row_tile(c_t[b][:, :, cols], PAIR), in1=factor, op=ALU.mult
+            )
+
+        def make_y2(b, cols, y):
+            nc.vector.tensor_tensor(
+                out=by_word(y, PAIR), in0=by_row_tile(a_t[b][:, :, cols], PAIR),
+                in1=by_row_tile(mat_t[b][:, :, cols], PAIR), op=ALU.mult,
+            )
+
+        def quantise_y(b, which, cols, y):
+            nc.vector.quantize_mx(out=y_code[b][:, which, cols].bitcast(E4M3), scales=y_scale[b][:, which, cols], in_=y)
+
+        whole = slice(0, PICK)
+        halves = [slice(0, HALF), slice(HALF, PICK)]
+        all_tiles = slice(0, PACK)
+
+        for t in range(PACK):
+            look(0, t, whole)
+            stronger(0, slice(t, t + 1), whole)
+        y_group0 = stage.tile([P, 2, PACK * PICK], BF16, name="y_group0", offset=AT_EARLY, align_bytes=64)
+        make_y2(0, whole, y_group0[:, 1, :])
+        make_y1(0, whole, y_group0[:, 0, :])
+        quantise_y(0, 1, whole, y_group0[:, 1, :])
+        quantise_y(0, 0, whole, y_group0[:, 0, :])
+
+        w3_code = keep.tile([P, 2, N], U32, name="w3_code", align_bytes=64)
+        w3_scale = keep.tile([P, 2, N], U8, name="w3_scale", align_bytes=64)
+        w3_rounded = [
+            stage.tile([P, PACK * N], BF16, name="w3_rounded%d" % b, offset=AT_LATE + 4 * KB * b, align_bytes=64)
+            for b in range(2)
         ]
-        yc, ysc = {}, {}
-        WALK = 2
-
-        def looks(b, u):
-            for t in range(PACK):
-                j = PACK * b + t
-                nc.scalar.activation(
-                    out=a_t[b][:, t, HALF * u : HALF * (u + 1)], in_=h_t[j][:].indirect(pos1_t[:, 16 * u : 16 * (u + 1)]),
-                    func=ACT.Sigmoid, bias=bias_t[:, j : j + 1], scale=slope_t[:, j : j + 1],
-                )
-
-        def signals(b, u):
-            cols = slice(HALF * u, HALF * (u + 1))
-            ys = ring.tile([P, 2, PACK * HALF], BF16, name="ys", tag="grouped", align_bytes=64)
-            walk = "p t (c i) -> p c t i"
-            yc[b, u] = keep.tile([P, 2, HALF], U32, name="yc%d%d" % (b, u), align_bytes=64)
-            ysc[b, u] = keep.tile([P, 2, HALF], U8, name="ysc%d%d" % (b, u), align_bytes=64)
-            nc.vector.tensor_tensor(
-                out=ys[:, 1, :].rearrange("p (c i t) -> p c t i", i=WALK, t=PACK),
-                in0=a_t[b][:, :, cols].rearrange(walk, i=WALK), in1=mat_t[b][:, :, cols].rearrange(walk, i=WALK),
-                op=ALU.mult,
-            )
-            nc.vector.tensor_tensor(out=c_t[b][:, :, cols], in0=a_t[b][:, :, cols], in1=c_t[b][:, :, cols], op=ALU.max)
-            nc.vector.quantize_mx(out=yc[b, u][:, 1, :].bitcast(E4M3), scales=ysc[b, u][:, 1, :], in_=ys[:, 1, :])
-            nc.vector.tensor_tensor(
-                out=ys[:, 0, :].rearrange("p (c i t) -> p c t i", i=WALK, t=PACK),
-                in0=c_t[b][:, :, cols].rearrange(walk, i=WALK),
-                in1=sv_t[:, PACK * b : PACK * (b + 1)].unsqueeze(1).unsqueeze(3).to_broadcast([P, HALF // WALK, PACK, WALK]),
-                op=ALU.mult,
-            )
-            nc.vector.quantize_mx(out=yc[b, u][:, 0, :].bitcast(E4M3), scales=ysc[b, u][:, 0, :], in_=ys[:, 0, :])
-
-        for u in range(2):
-            looks(0, u)
-            signals(0, u)
-        for j in range(4, 8):
-            h_tile(j, nc.scalar.copy)
-        for u in range(2):
-            looks(1, u)
-        signals(1, 0)
-
-        w3c, w3s = [], []
         for b in range(2):
-            grouped3 = hs.tile([P, PACK * N], BF16, name="grouped3%d" % b, offset=4 * S * (6 + b), align_bytes=64)
-            nc.scalar.copy(
-                out=grouped3[:].rearrange("p (c i j) -> p c j i", i=WALK, j=PACK),
-                in_=w3raw[b][:].rearrange("p j (c i) -> p c j i", i=WALK),
+            nc.vector.tensor_copy(out=by_word(w3_rounded[b][:], PAIR), in_=by_row_tile(w3_raw[b][:], PAIR))
+        for b in range(2):
+            nc.vector.quantize_mx(out=w3_code[:, b, :].bitcast(E4M3), scales=w3_scale[:, b, :], in_=w3_rounded[b][:])
+
+        for j in range(PACK, 2 * PACK):
+            h_tile(j, nc.scalar.copy)
+        for cols in halves:
+            for t in range(PACK):
+                look(1, t, cols)
+        y_half = [
+            stage.tile([P, 2, PACK * HALF], BF16, name="y_half%d" % u, offset=AT_LATE + 4 * KB * u, align_bytes=64)
+            for u in range(2)
+        ]
+        stronger(1, all_tiles, halves[0])
+        make_y2(1, halves[0], y_half[0][:, 1, :])
+        stronger(1, all_tiles, halves[1])
+        y1_tiles = keep.tile([P, PACK, HALF], BF16, name="y1_tiles")
+        for t in range(PACK):
+            nc.scalar.activation(
+                out=y1_tiles[:, t, :], in_=c_t[1][:, t, halves[1]], func=ACT.Copy, scale=sv_t[:, PACK + t : PACK + t + 1]
             )
-            w3c.append(keep.tile([P, N], U32, name="w3c%d" % b, align_bytes=64))
-            w3s.append(keep.tile([P, N], U8, name="w3s%d" % b, align_bytes=64))
-            nc.vector.quantize_mx(out=w3c[b][:].bitcast(E4M3), scales=w3s[b][:], in_=grouped3[:])
-        signals(1, 1)
+        nc.scalar.copy(out=by_word(y_half[1][:, 0, :], 4), in_=by_row_tile(y1_tiles[:], 4))
+        make_y1(1, halves[0], y_half[0][:, 0, :])
+        quantise_y(1, 1, halves[0], y_half[0][:, 1, :])
+        quantise_y(1, 0, halves[0], y_half[0][:, 0, :])
+        make_y2(1, halves[1], y_half[1][:, 1, :])
+        quantise_y(1, 0, halves[1], y_half[1][:, 0, :])
+        quantise_y(1, 1, halves[1], y_half[1][:, 1, :])
+
+        shares = [[0, 1], [2]]
+        weights = [(w3_code, w3_scale), (w4_code, w4_scale)]
+        sums = {}
+        for u in range(2):
+            for which in range(2):
+                for x in range(len(shares)):
+                    sums[u, which, x] = psum.tile([P, BANK], F32, name="sums%d%d%d" % (u, which, x), tag="bank")
+
+        def second_stage(b, u):
+            for which, (code, scale) in enumerate(weights):
+                for x, share in enumerate(shares):
+                    for place, k in enumerate(share):
+                        nc.tensor.matmul_mx(
+                            out=sums[u, which, x][:, HALF * place : HALF * (place + 1)],
+                            lhsT=code[:, b, P * k : P * (k + 1)].bitcast(E4M3),
+                            lhsT_scale=scale[:, b, P * k : P * (k + 1)],
+                            rhs=y_code[b][:, which, halves[u]].bitcast(E4M3),
+                            rhs_scale=y_scale[b][:, which, halves[u]],
+                            start=(b == 0 and place == 0), stop=(b == 1 and place == len(share) - 1),
+                        )
 
         for u in range(2):
-            result = [psum.tile([P, BANK], F32, name="res%d%d" % (u, k), tag="bank") for k in range(3)]
-            for b in range(2):
-                for k in range(3):
-                    rows = slice(P * k, P * (k + 1))
-                    nc.tensor.matmul_mx(
-                        out=result[k][:, HALF:BANK], lhsT=w4c[:, b, rows].bitcast(E4M3), lhsT_scale=w4s[:, b, rows],
-                        rhs=yc[b, u][:, 1, :].bitcast(E4M3), rhs_scale=ysc[b, u][:, 1, :], start=(b == 0), stop=False,
-                    )
-            for b in range(2):
-                for k in range(3):
-                    rows = slice(P * k, P * (k + 1))
-                    nc.tensor.matmul_mx(
-                        out=result[k][:, 0:HALF], lhsT=w3c[b][:, rows].bitcast(E4M3), lhsT_scale=w3s[b][:, rows],
-                        rhs=yc[b, u][:, 0, :].bitcast(E4M3), rhs_scale=ysc[b, u][:, 0, :], start=False, stop=(b == 1),
-                    )
-            for k in range(3):
-                bounded = keep.tile([P, HALF], F32, name="bounded%d%d" % (u, k))
-                nc.scalar.activation(out=bounded[:], in_=result[k][:, 0:HALF], func=ACT.Tanh)
-                nc.vector.tensor_tensor(out=bounded[:], in0=result[k][:, HALF:BANK], in1=bounded[:], op=ALU.add)
-                nc.sync.dma_start(out=out[P * k : P * (k + 1), HALF * u : HALF * (u + 1)], in_=bounded[:])
+            second_stage(0, u)
+        for u in range(2):
+            second_stage(1, u)
+            for x, share in enumerate(shares):
+                width = HALF * len(share)
+                result = keep.tile([P, width], F32, name="result%d%d" % (u, x))
+                nc.scalar.activation(out=result[:], in_=sums[u, 0, x][:, 0:width], func=ACT.Tanh)
+                nc.vector.tensor_tensor(out=result[:], in0=sums[u, 1, x][:, 0:width], in1=result[:], op=ALU.add)
+                nc.sync.dma_start(
+                    out=out[P * share[0] : P * (share[-1] + 1), halves[u]].rearrange("(k p) c -> p k c", p=P),
+                    in_=result[:].rearrange("p (k c) -> p k c", c=HALF),
+                )

from contextlib import ExitStack

import concourse.mybir as mybir

K, H, N, T, S, PICK = 1024, 1024, 384, 2048, 1024, 512
FLOPS = 2 * (2 * K * H * S + 2 * H * N * PICK)

F32 = mybir.dt.float32
BF16 = mybir.dt.bfloat16
I32 = mybir.dt.int32
U32 = mybir.dt.uint32
U16 = mybir.dt.uint16
U8 = mybir.dt.uint8
E4M3 = mybir.dt.float8_e4m3fn_x4
E2M1 = mybir.dt.float4_e2m1fn_x4
ALU = mybir.AluOpType
ACT = mybir.ActivationFunctionType

P = 128
PACK = 4
KP = P * PACK
BANK = 512
HALF = PICK // 2
PER_COLUMN = 16
LIVE = 24
MOVED = 100
KB = 1024

AT_TAB_WORDS = [0, 8 * KB]
AT_TAB_SCALES = 27 * KB
AT_W2_WORDS = 44 * KB
AT_W2_SCALES = 52 * KB
AT_PICKED_SCALES = 54 * KB
AT_W1 = {(0, 0): 20 * KB, (1, 0): 28 * KB, (0, 1): AT_TAB_WORDS[0], (1, 1): AT_TAB_WORDS[1]}
AT_W3 = [40 * KB, 46 * KB]
AT_W4_SCALES = AT_PICKED_SCALES
AT_W4_WORDS = AT_W1[0, 1]
AT_C0 = 16 * KB
AT_MAT = [24 * KB, 32 * KB]
AT_G = [4 * KB * j for j in range(7)] + [34 * KB]
AT_A = [28 * KB, 36 * KB]
AT_H = [44 * KB + 4 * KB * j for j in range(3)] + [58 * KB, 56 * KB, 60 * KB, 64 * KB, 68 * KB]
AT_EARLY = 0
AT_LATE = 8 * KB
AT_W1_CODES = [AT_LATE, 16 * KB]
AT_W2_DEALT = [20 * KB, AT_LATE]


def tile_list_evacuation_drill_reading_kernel(
    tc, tab_words, tab_scales, offs, pos1, pos2, w1, w2_words, w2_scales, w3,
    w4_words, w4_scales, gam, slope, bias, temp, sv, mat, out,
):
    nc = tc.nc
    with ExitStack() as ctx:
        keep = ctx.enter_context(tc.tile_pool(name="keep", bufs=1))
        rows = ctx.enter_context(tc.tile_pool(name="rows", bufs=1))
        loads = ctx.enter_context(tc.tile_pool(name="loads", bufs=1))
        stage = ctx.enter_context(tc.tile_pool(name="stage", bufs=1))
        psum = ctx.enter_context(tc.psum_pool(name="psum", bufs=8))

        def load_list(src, name):
            tile = keep.tile(list(src.shape), U16, name=name)
            nc.sync.dma_start(tile[:], src)
            return tile

        def load_per_row(vec, name):
            tile = keep.tile([P, 2 * PACK], F32, name=name)
            nc.gpsimd.dma_start(
                out=tile[:].rearrange("p (b t) -> p b t", b=2), in_=vec.rearrange("(b p t) -> p b t", b=2, t=PACK)
            )
            return tile

        def load_scales(tile, src):
            for q in range(4):
                nc.sync.dma_start(
                    out=tile[32 * q : 32 * q + 4, :, :].bitcast(I32),
                    in_=src[:, 4 * q : 4 * q + 4, :].rearrange("a s e -> s a e").bitcast(I32),
                )

        def load_pass(src, name, offset):
            tile = loads.tile([P, PACK, src.shape[1]], F32, name=name, offset=offset)
            nc.sync.dma_start(out=tile[:], in_=src.rearrange("(p i) c -> p i c", i=PACK))
            return tile

        offs_t = load_list(offs, "offs_t")
        tab_s = loads.tile([P, T], U8, name="tab_s", offset=AT_TAB_SCALES)
        for q in range(4):
            nc.sync.dma_start(
                out=tab_s[32 * q + LIVE : 32 * q + 32, :].bitcast(I32),
                in_=tab_scales[:, 4 * q : 4 * q + 4, :].bitcast(I32),
            )
        w2_s = loads.tile([P, 2, H], U8, name="w2_s", offset=AT_W2_SCALES)
        nc.gpsimd.memset(w2_s[:].bitcast(I32), 0)
        for q in range(4):
            engine = nc.vector if q < 3 else nc.gpsimd
            engine.memset(tab_s[32 * q : 32 * q + LIVE, :].bitcast(I32), 0)
        v_scales = [keep.tile([P, S], U8, name="v_scales%d" % a, align_bytes=64) for a in range(2)]
        for a in range(2):
            nc.gpsimd.memset(v_scales[a][96:P, :].bitcast(I32), 0)
        tab_w = [loads.tile([P, T], U32, name="tab_w%d" % a, offset=AT_TAB_WORDS[a], align_bytes=64) for a in range(2)]

        def load_words(a):
            nc.sync.dma_start(
                out=tab_w[a][:].bitcast(I32), in_=tab_words[a].rearrange("p t i -> p (t i)").bitcast(I32)
            )

        load_words(0)
        load_scales(w2_s, w2_scales)
        load_words(1)
        w2_w = loads.tile([P, 2, 2 * H], U8, name="w2_w", offset=AT_W2_WORDS)
        nc.sync.dma_start(out=w2_w[:].bitcast(I32), in_=w2_words.rearrange("a p e -> p a e").bitcast(I32))
        pos2_t = load_list(pos2, "pos2_t")
        pos1_t = load_list(pos1, "pos1_t")
        gam_t = load_per_row(gam, "gam_t")
        temp_t = load_per_row(temp, "temp_t")
        slope_t = load_per_row(slope, "slope_t")
        bias_t = load_per_row(bias, "bias_t")
        sv_t = load_per_row(sv, "sv_t")

        picked_s = loads.tile([P, S], U8, name="picked_s", offset=AT_PICKED_SCALES)
        nc.vector.tensor_copy(picked_s[:], tab_s[:].indirect(offs_t[:]))
        for a in range(2):
            first = LIVE + 4 * a
            nc.sync.dma_start(
                out=v_scales[a][0:MOVED, :].bitcast(I32), in_=picked_s[first : first + MOVED, :].bitcast(I32)
            )
        v_words = [keep.tile([P, S], U32, name="v_words%d" % a, align_bytes=64) for a in range(2)]
        w2_scale = [keep.tile([P, 2, KP], U8, name="w2_scale%d" % b, align_bytes=64) for b in range(2)]

        def deal_w2_scales(b):
            nc.vector.tensor_copy(
                out=w2_scale[b][:].rearrange("p a (t m i) -> p a m t i", t=PACK, i=16),
                in_=w2_s[:, :, KP * b : KP * (b + 1)].rearrange("p a (m i t) -> p a m t i", t=PACK, i=16),
            )

        nc.vector.tensor_copy(v_words[0][:], tab_w[0][:].indirect(offs_t[:]))
        deal_w2_scales(0)
        for n in range(2):
            entries = slice(BANK * n // PER_COLUMN, BANK * (n + 1) // PER_COLUMN)
            nc.vector.tensor_copy(v_words[1][:, BANK * n : BANK * (n + 1)], tab_w[1][:].indirect(offs_t[:, entries]))
        deal_w2_scales(1)

        w2_code = {}
        for b in range(2):
            for a in range(2):
                w2_code[a, b] = stage.tile(
                    [P, 2 * KP], U8, name="w2_code%d%d" % (a, b), offset=AT_W2_DEALT[b] + KB * a, align_bytes=64
                )
                nc.scalar.copy(
                    out=w2_code[a, b][:].bitcast(U16).rearrange("p (t m i) -> p m t i", t=PACK, i=8),
                    in_=w2_w[:, a, 2 * KP * b : 2 * KP * (b + 1)].bitcast(U16).rearrange(
                        "p (m i t) -> p m t i", t=PACK, i=8
                    ),
                )

        w1_raw = {}
        for b in range(2):
            for a in range(2):
                block = w1[KP * a : KP * (a + 1), KP * b : KP * (b + 1)]
                w1_raw[a, b] = load_pass(block, "w1_raw%d%d" % (a, b), AT_W1[a, b])
        w3_raw = [load_pass(w3[KP * b : KP * (b + 1), :], "w3_raw%d" % b, AT_W3[b]) for b in range(2)]
        w4_scale = loads.tile([P, 2, N], U8, name="w4_scale", offset=AT_W4_SCALES)
        nc.gpsimd.memset(w4_scale[:].bitcast(I32), 0)
        load_scales(w4_scale, w4_scales)
        minus_temp = keep.tile([P, 2 * PACK], F32, name="minus_temp")
        nc.gpsimd.tensor_scalar(out=minus_temp[:], in0=temp_t[:], scalar1=-1.0, scalar2=0.0, op0=ALU.mult, op1=ALU.add)

        def first_stage(codes, scales, n):
            bank = psum.tile([P, BANK], F32, name="bank", tag="bank")
            cols = slice(BANK * n, BANK * (n + 1))
            for a in range(2):
                nc.tensor.matmul_mx(
                    out=bank[:], lhsT=codes[a], lhsT_scale=scales[a],
                    rhs=v_words[a][:, cols].bitcast(E4M3), rhs_scale=v_scales[a][:, cols],
                    start=(a == 0), stop=(a == 1),
                )
            return bank

        bank_max = keep.tile([P, 2 * 2 * PACK], F32, name="bank_max")
        exp_bias = keep.tile([P, 2 * PACK], F32, name="exp_bias")
        c_t = [loads.tile([P, PACK, PICK], F32, name="c0", offset=AT_C0), keep.tile([P, PACK, PICK], F32, name="c1")]

        def g_tile(j):
            b, t = divmod(j, PACK)
            g = rows.tile([P, S], F32, name="g%d" % j, offset=AT_G[j])
            for n in range(2):
                bank = first_stage(
                    [w2_code[a, b][:, 2 * P * t : 2 * P * (t + 1)].bitcast(E2M1) for a in range(2)],
                    [w2_scale[b][:, a, P * t : P * (t + 1)] for a in range(2)], n,
                )
                nc.vector.tensor_scalar(
                    out=g[:, BANK * n : BANK * (n + 1)], in0=bank[:], scalar1=gam_t[:, j : j + 1], scalar2=None,
                    op0=ALU.mult, op1=ALU.max, accum_out=bank_max[:, 2 * j + n : 2 * j + n + 1],
                )
            nc.gpsimd.tensor_scalar(
                out=exp_bias[:, j : j + 1], in0=bank_max[:, 2 * j : 2 * j + 1],
                scalar1=bank_max[:, 2 * j + 1 : 2 * j + 2], scalar2=minus_temp[:, j : j + 1],
                op0=ALU.max, op1=ALU.mult,
            )
            nc.scalar.activation(
                out=c_t[b][:, t, :], in_=g[:].indirect(pos2_t[:]), func=ACT.Exp,
                bias=exp_bias[:, j : j + 1], scale=temp_t[:, j : j + 1],
            )

        def round_w1(b, copy):
            rounded = stage.tile(
                [P, 2, PACK * KP], BF16, name="w1_rounded%d" % b, offset=[AT_EARLY, AT_LATE][b], align_bytes=64
            )
            for a in range(2):
                dst = rounded[:, a, :].rearrange("p (u v m i) -> p u m i v", u=2, v=2, i=PACK)
                src = w1_raw[a, b][:].rearrange("p i (m u v) -> p u m i v", u=2, v=2)
                for u in range(2):
                    copy(out=dst[:, u], in_=src[:, u])
            return rounded

        w1_code, w1_scale = {}, {}

        def quantise_w1(b, rounded):
            w1_code[b] = stage.tile([P, 2, KP], U32, name="w1_code%d" % b, offset=AT_W1_CODES[b], align_bytes=64)
            w1_scale[b] = keep.tile([P, 2, KP], U8, name="w1_scale%d" % b, align_bytes=64)
            nc.vector.quantize_mx(
                out=w1_code[b][:].rearrange("p a c -> p (a c)").bitcast(E4M3),
                scales=w1_scale[b][:].rearrange("p a c -> p (a c)"),
                in_=rounded[:].rearrange("p a c -> p (a c)"),
            )

        h_t = {}

        def h_tile(j, copy):
            b, t = divmod(j, PACK)
            h_t[j] = rows.tile([P, S], F32, name="h%d" % j, offset=AT_H[j])
            for n in range(2):
                bank = first_stage(
                    [w1_code[b][:, a, P * t : P * (t + 1)].bitcast(E4M3) for a in range(2)],
                    [w1_scale[b][:, a, P * t : P * (t + 1)] for a in range(2)], n,
                )
                copy(out=h_t[j][:, BANK * n : BANK * (n + 1)], in_=bank[:])

        w1_rounded = round_w1(0, nc.scalar.copy)
        for j in range(PACK):
            g_tile(j)
        mat_t = [load_pass(mat[KP * b : KP * (b + 1), :], "mat%d" % b, AT_MAT[b]) for b in range(2)]
        for j in range(PACK, 2 * PACK):
            g_tile(j)
        quantise_w1(0, w1_rounded)
        for j in range(PACK):
            h_tile(j, nc.vector.tensor_copy)
        quantise_w1(1, round_w1(1, nc.vector.tensor_copy))
        w4_code = loads.tile([P, 2, N], U32, name="w4_code", offset=AT_W4_WORDS)
        nc.sync.dma_start(out=w4_code[:].bitcast(I32), in_=w4_words.rearrange("a p e i -> p a (e i)").bitcast(I32))

        a_t = [rows.tile([P, PACK, PICK], F32, name="a%d" % b, offset=AT_A[b]) for b in range(2)]
        y_code = [keep.tile([P, 2, PICK], U32, name="y_code%d" % b, align_bytes=64) for b in range(2)]
        y_scale = [keep.tile([P, 2, PICK], U8, name="y_scale%d" % b, align_bytes=64) for b in range(2)]

        def by_row_tile(ap, run):
            return ap.rearrange("p t (c i) -> p c t i", i=run)

        def by_word(ap, run):
            return ap.rearrange("p (c i t) -> p c t i", i=run, t=PACK)

        PAIR = 2

        def look(b, t, cols):
            j = PACK * b + t
            entries = slice(cols.start // PER_COLUMN, cols.stop // PER_COLUMN)
            nc.scalar.activation(
                out=a_t[b][:, t, cols], in_=h_t[j][:].indirect(pos1_t[:, entries]), func=ACT.Sigmoid,
                bias=bias_t[:, j : j + 1], scale=slope_t[:, j : j + 1],
            )

        def stronger(b, tiles, cols):
            nc.vector.tensor_tensor(
                out=c_t[b][:, tiles, cols], in0=a_t[b][:, tiles, cols], in1=c_t[b][:, tiles, cols], op=ALU.max
            )

        def make_y1(b, cols, y):
            count = (cols.stop - cols.start) // PAIR
            factor = sv_t[:, PACK * b : PACK * (b + 1)].unsqueeze(1).unsqueeze(3).to_broadcast([P, count, PACK, PAIR])
            nc.vector.tensor_tensor(
                out=by_word(y, PAIR), in0=by_row_tile(c_t[b][:, :, cols], PAIR), in1=factor, op=ALU.mult
            )

        def make_y2(b, cols, y):
            nc.vector.tensor_tensor(
                out=by_word(y, PAIR), in0=by_row_tile(a_t[b][:, :, cols], PAIR),
                in1=by_row_tile(mat_t[b][:, :, cols], PAIR), op=ALU.mult,
            )

        def quantise_y(b, which, cols, y):
            nc.vector.quantize_mx(out=y_code[b][:, which, cols].bitcast(E4M3), scales=y_scale[b][:, which, cols], in_=y)

        whole = slice(0, PICK)
        halves = [slice(0, HALF), slice(HALF, PICK)]
        all_tiles = slice(0, PACK)

        for t in range(PACK):
            look(0, t, whole)
            stronger(0, slice(t, t + 1), whole)
        y_group0 = stage.tile([P, 2, PACK * PICK], BF16, name="y_group0", offset=AT_EARLY, align_bytes=64)
        make_y2(0, whole, y_group0[:, 1, :])
        make_y1(0, whole, y_group0[:, 0, :])
        quantise_y(0, 1, whole, y_group0[:, 1, :])
        quantise_y(0, 0, whole, y_group0[:, 0, :])

        w3_code = keep.tile([P, 2, N], U32, name="w3_code", align_bytes=64)
        w3_scale = keep.tile([P, 2, N], U8, name="w3_scale", align_bytes=64)
        w3_rounded = [
            stage.tile([P, PACK * N], BF16, name="w3_rounded%d" % b, offset=AT_LATE + 4 * KB * b, align_bytes=64)
            for b in range(2)
        ]
        for b in range(2):
            nc.vector.tensor_copy(out=by_word(w3_rounded[b][:], PAIR), in_=by_row_tile(w3_raw[b][:], PAIR))
        for b in range(2):
            nc.vector.quantize_mx(out=w3_code[:, b, :].bitcast(E4M3), scales=w3_scale[:, b, :], in_=w3_rounded[b][:])

        for j in range(PACK, 2 * PACK):
            h_tile(j, nc.scalar.copy)
        for cols in halves:
            for t in range(PACK):
                look(1, t, cols)
        y_half = [
            stage.tile([P, 2, PACK * HALF], BF16, name="y_half%d" % u, offset=AT_LATE + 4 * KB * u, align_bytes=64)
            for u in range(2)
        ]
        stronger(1, all_tiles, halves[0])
        make_y2(1, halves[0], y_half[0][:, 1, :])
        stronger(1, all_tiles, halves[1])
        y1_tiles = keep.tile([P, PACK, HALF], BF16, name="y1_tiles")
        for t in range(PACK):
            nc.scalar.activation(
                out=y1_tiles[:, t, :], in_=c_t[1][:, t, halves[1]], func=ACT.Copy, scale=sv_t[:, PACK + t : PACK + t + 1]
            )
        nc.scalar.copy(out=by_word(y_half[1][:, 0, :], 4), in_=by_row_tile(y1_tiles[:], 4))
        make_y1(1, halves[0], y_half[0][:, 0, :])
        quantise_y(1, 1, halves[0], y_half[0][:, 1, :])
        quantise_y(1, 0, halves[0], y_half[0][:, 0, :])
        make_y2(1, halves[1], y_half[1][:, 1, :])
        quantise_y(1, 0, halves[1], y_half[1][:, 0, :])
        quantise_y(1, 1, halves[1], y_half[1][:, 1, :])

        shares = [[0, 1], [2]]
        weights = [(w3_code, w3_scale), (w4_code, w4_scale)]
        sums = {}
        for u in range(2):
            for which in range(2):
                for x in range(len(shares)):
                    sums[u, which, x] = psum.tile([P, BANK], F32, name="sums%d%d%d" % (u, which, x), tag="bank")

        def second_stage(b, u):
            for which, (code, scale) in enumerate(weights):
                for x, share in enumerate(shares):
                    for place, k in enumerate(share):
                        nc.tensor.matmul_mx(
                            out=sums[u, which, x][:, HALF * place : HALF * (place + 1)],
                            lhsT=code[:, b, P * k : P * (k + 1)].bitcast(E4M3),
                            lhsT_scale=scale[:, b, P * k : P * (k + 1)],
                            rhs=y_code[b][:, which, halves[u]].bitcast(E4M3),
                            rhs_scale=y_scale[b][:, which, halves[u]],
                            start=(b == 0 and place == 0), stop=(b == 1 and place == len(share) - 1),
                        )

        for u in range(2):
            second_stage(0, u)
        for u in range(2):
            second_stage(1, u)
            for x, share in enumerate(shares):
                width = HALF * len(share)
                result = keep.tile([P, width], F32, name="result%d%d" % (u, x))
                nc.scalar.activation(out=result[:], in_=sums[u, 0, x][:, 0:width], func=ACT.Tanh)
                nc.vector.tensor_tensor(out=result[:], in0=sums[u, 1, x][:, 0:width], in1=result[:], op=ALU.add)
                nc.sync.dma_start(
                    out=out[P * share[0] : P * (share[-1] + 1), halves[u]].rearrange("(k p) c -> p k c", p=P),
                    in_=result[:].rearrange("p (k c) -> p k c", c=HALF),
                )
